import numpy as np
import ml_dtypes


def mxq(x, axis, fmt="e4m3"):
    dtype, down = {"e4m3": (ml_dtypes.float8_e4m3fn, 7), "e5m2": (ml_dtypes.float8_e5m2, 14)}[fmt]
    v = np.moveaxis(np.asarray(x, np.float32).astype(ml_dtypes.bfloat16).astype(np.float64), axis, -1)
    blocks = v.reshape(v.shape[:-1] + (-1, 32))
    amax = np.abs(blocks).max(-1, keepdims=True)
    byte = np.maximum(np.where(amax > 0, np.frexp(amax)[1] - 1 + 127, 0) - down, 1)
    scale = np.exp2(byte - 127.0)
    codes = (blocks / scale).astype(np.float32).astype(dtype).astype(np.float64)
    return np.moveaxis((codes * scale).reshape(v.shape), -1, axis)


WIDE = False


def mx_kscale(k):
    if not WIDE:
        return np.ones(k)
    levels = np.array([10, -10, 5, -5, 0])
    if k % 512:
        return np.exp2(np.random.permutation(np.resize(levels, k // 32))).repeat(32)
    a = np.empty((k // 512, 16))
    for p in range(k // 512):
        a[p, :8] = np.random.permutation(np.resize(levels, 8))
        for g in range(8):
            far = levels[np.abs(levels - a[p, g]) >= 10]
            a[p, g + 8] = far[np.random.randint(len(far))]
    return np.exp2(a.ravel()).repeat(32)


def f64(x):
    return np.asarray(x).astype(np.float64)


def striped(idx):
    return np.tile(idx.reshape(-1, 16).T, (8, 1)).astype(np.uint16)


def unstriped(offs):
    return offs[:16].T.reshape(-1).astype(np.int64)


E2M1 = np.array([0.0, 0.5, 1.0, 1.5, 2.0, 3.0, 4.0, 6.0, -0.0, -0.5, -1.0, -1.5, -2.0, -3.0, -4.0, -6.0])


def pack_weight(w, fmt):
    k, n = w.shape
    w = f64(np.asarray(w, np.float32).astype(ml_dtypes.bfloat16)).reshape(k // 32, 32, n)
    amax = np.abs(w).max(1)
    if fmt == "e4m3":
        byte = np.frexp(amax)[1] - 1 + 127 - 7
    else:
        mant, ex = np.frexp(amax / 6.0)
        byte = np.where(mant > 0.5, ex, ex - 1) + 127
    byte = np.clip(np.where(amax > 0, byte, 1), 1, 254)
    scaled = (w * np.exp2(127.0 - byte)[:, None, :]).reshape(k, n).astype(np.float32)
    by_word = np.ascontiguousarray(scaled.reshape(k // 512, 128, 4, n).transpose(0, 1, 3, 2))
    if fmt == "e4m3":
        words = by_word.astype(ml_dtypes.float8_e4m3fn).view(np.uint8)
    else:
        c = by_word.astype(ml_dtypes.float4_e2m1fn).view(np.uint8) & 0xF
        words = (c[..., 0::2] | (c[..., 1::2] << 4)).reshape(k // 512, 128, 2 * n)
    return np.ascontiguousarray(words), np.ascontiguousarray(byte.astype(np.uint8).reshape(k // 512, 16, n))


def unpack_weight(words, scales, fmt):
    g, _, n = scales.shape
    words = np.ascontiguousarray(words).reshape(g, 128, n, -1)
    if fmt == "e4m3":
        vals = words.view(ml_dtypes.float8_e4m3fn).astype(np.float64)
    else:
        nib = np.empty((g, 128, n, 4), np.uint8)
        nib[..., 0::2] = words & 0xF
        nib[..., 1::2] = words >> 4
        vals = E2M1[nib]
    vals = vals * np.repeat(np.exp2(scales.astype(np.float64) - 127.0), 8, axis=1)[..., None]
    return vals.transpose(0, 1, 3, 2).reshape(g * 512, n)


def gelu(v):
    return 0.5 * v * (1.0 + np.tanh(np.sqrt(2.0 / np.pi) * (v + 0.044715 * v**3)))


def twice(P):
    return np.random.permutation(np.repeat(np.arange(P), 2))


K, T, S, H, P = 1536, 4096, 1024, 512, 512

def setup_inputs():
    n = np.random.standard_normal
    s = mx_kscale(K)[:, None]
    u = mx_kscale(H)[:, None]
    d = {}
    d["tab_words"], d["tab_scales"] = pack_weight(n((K, T)) * s, "e4m3")
    d["offs"] = striped(np.random.permutation(T)[:S])
    d["w1"] = (n((K, H)) / s / K ** 0.5).astype(np.float32)
    d["gain"] = (np.random.uniform(0.85, 1.15, H) * u[:, 0]).astype(np.float32)
    d["pos1"] = striped(np.random.permutation(S)[:P])
    d["pos2"] = striped(np.random.permutation(S)[:P])
    d["w4_words"], d["w4_scales"] = pack_weight(0.58 * n((H, H)) / u / H ** 0.5, "e2m1")
    d["pos3"] = striped(twice(P))
    d["back"] = (np.sign(n(H)) * np.random.uniform(0.48, 0.56, H) / u[:, 0]).astype(np.float32)
    return d

def reference(tab_words, tab_scales, offs, w1, gain, pos1, pos2, w4_words, w4_scales, pos3, back):
    v = unpack_weight(tab_words, tab_scales, "e4m3")[:, unstriped(offs)]
    e = mxq(f64(w1), 0, "e4m3").T @ v
    h = 0.5 * e * (1.0 + np.tanh((2.0 / np.pi) ** 0.5 * (e + 0.044715 * e ** 3))) * f64(gain)[:, None]
    x = h[:, unstriped(pos1)] + h[:, unstriped(pos2)]
    w4 = unpack_weight(w4_words, w4_scales, "e2m1")
    y = w4.T @ mxq(x, 0, "e4m3")
    yu = y[:, unstriped(pos3)]
    hs = f64(back)[:, None] * h
    out = hs * np.sin(yu) + yu * np.cos(hs)
    return out

@@ -1,0 +1,267 @@
+import math
+from contextlib import ExitStack
+
+import concourse.mybir as mybir
+
+K, T, S, H, PAIRS = 1536, 4096, 1024, 512, 512
+FLOPS = 2 * K * H * S + 2 * H * H * PAIRS
+
+F32 = mybir.dt.float32
+BF16 = mybir.dt.bfloat16
+I32 = mybir.dt.int32
+U32 = mybir.dt.uint32
+U16 = mybir.dt.uint16
+U8 = mybir.dt.uint8
+FP8X4 = mybir.dt.float8_e4m3fn_x4
+FP4X4 = mybir.dt.float4_e2m1fn_x4
+ACT = mybir.ActivationFunctionType
+ALU = mybir.AluOpType
+
+P = 128
+PACK = 4
+PASSES = K // (P * PACK)
+BANK = 512
+
+
+def tile_list_slewing_play_features_kernel(
+    tc, tab_words, tab_scales, offs, w1, gain, pos1, pos2, w4_words, w4_scales, pos3, back, out
+):
+    nc = tc.nc
+    with ExitStack() as ctx:
+        keep = ctx.enter_context(tc.tile_pool(name="keep", bufs=1))
+        psum = ctx.enter_context(tc.psum_pool(name="psum", bufs=1))
+        work = ctx.enter_context(tc.tile_pool(name="work", bufs=2))
+
+        def held(shape, dtype, name):
+            return keep.tile(shape, dtype, name=name, align_bytes=64)
+
+        idx = held([P, S // 16], U16, "idx")
+        p1 = held([P, PAIRS // 16], U16, "p1")
+        p2 = held([P, PAIRS // 16], U16, "p2")
+        p3 = held([P, S // 16], U16, "p3")
+        tab_w = [keep.tile([P, T], U32, name=f"tab_w{a}", tag=f"tab_w{a}", align_bytes=64) for a in range(PASSES)]
+        tab_s = held([P, T], U8, "tab_s")
+        w1_raw = [held([P, PACK, H], F32, f"w1_raw{a}") for a in range(PASSES)]
+        gain_sb = held([P, PACK], F32, "gain_sb")
+        back_sb = held([P, PACK], F32, "back_sb")
+        w4_w_raw = held([P, 2 * H], U8, "w4_w_raw")
+        w4_s_raw = held([P, H], U8, "w4_s_raw")
+
+        nc.vector.memset(tab_s[:].bitcast(I32), 0)
+        nc.vector.memset(w4_s_raw[:].bitcast(I32), 0)
+
+        def load_table(a):
+            nc.sync.dma_start(
+                out=tab_w[a][:].bitcast(I32), in_=tab_words[a].rearrange("p n i -> p (n i)").bitcast(I32)
+            )
+
+        def load_w1(a):
+            rows = w1[a * P * PACK : (a + 1) * P * PACK, :]
+            nc.sync.dma_start(out=w1_raw[a][:], in_=rows.rearrange("(p i) r -> p i r", i=PACK))
+
+        nc.sync.dma_start(idx[:], offs)
+        for q in range(4):
+            nc.scalar.dma_start(
+                out=tab_s[32 * q : 32 * q + 4 * PASSES, :].bitcast(I32),
+                in_=tab_scales[:, 4 * q : 4 * q + 4, :].bitcast(I32),
+            )
+        load_table(0)
+        load_w1(0)
+        nc.sync.dma_start(p1[:], pos1)
+        nc.sync.dma_start(p2[:], pos2)
+        nc.sync.dma_start(p3[:], pos3)
+        nc.sync.dma_start(out=gain_sb[:], in_=gain.rearrange("(p i) -> p i", i=PACK))
+        nc.sync.dma_start(out=back_sb[:], in_=back.rearrange("(p i) -> p i", i=PACK))
+        nc.sync.dma_start(out=w4_w_raw[:].bitcast(I32), in_=w4_words[0].bitcast(I32))
+        for q in range(4):
+            nc.sync.dma_start(
+                out=w4_s_raw[32 * q : 32 * q + 4, :].bitcast(I32),
+                in_=w4_scales[0, 4 * q : 4 * q + 4, :].bitcast(I32),
+            )
+        for a in range(1, PASSES):
+            load_table(a)
+            load_w1(a)
+
+        minus_half_pi = held([P, 1], F32, "minus_half_pi")
+        minus_pi = held([P, 1], F32, "minus_pi")
+        one = held([P, 1], F32, "one")
+        nc.vector.memset(one[:], 1.0)
+        nc.vector.tensor_scalar(minus_half_pi[:], one[:], -math.pi / 2, None, ALU.mult)
+        nc.vector.tensor_scalar(minus_pi[:], one[:], -math.pi, None, ALU.mult)
+
+        got_s = held([P, S], U8, "got_s")
+        nc.vector.tensor_copy(got_s[:], tab_s[:].indirect(idx[:]))
+        got_w = [held([P, S], U32, f"got_w{a}") for a in range(PASSES)]
+        w1_codes = [held([P, H], U32, f"w1_codes{a}") for a in range(PASSES)]
+        w1_scales = [held([P, H], U8, f"w1_scales{a}") for a in range(PASSES)]
+        banks = [[psum.tile([P, BANK], F32, name=f"e{i}_{c}", tag=f"bank{i}_{c}") for c in range(2)] for i in range(PACK)]
+
+        def multiply_first(a, i):
+            cols = slice(P * i, P * (i + 1))
+            for c in range(2):
+                ent = slice(BANK * c, BANK * (c + 1))
+                nc.tensor.matmul_mx(
+                    out=banks[i][c][:],
+                    lhsT=w1_codes[a][:, cols].bitcast(FP8X4),
+                    lhsT_scale=w1_scales[a][:, cols],
+                    rhs=got_w[a][:, ent].bitcast(FP8X4),
+                    rhs_scale=got_s[4 * a : P, ent],
+                    start=(a == 0),
+                    stop=(a == PASSES - 1),
+                )
+
+        bg = held([P, PACK], F32, "bg")
+        bg_neg = held([P, PACK], F32, "bg_neg")
+        bg_abs = held([P, PACK], F32, "bg_abs")
+        w4_w = held([P, 2 * H], U8, "w4_w")
+        w4_s = held([P, H], U8, "w4_s")
+
+        for a in range(PASSES):
+            nc.vector.tensor_copy(got_w[a][:], tab_w[a][:].indirect(idx[:]))
+            src = w1_raw[a][:].rearrange("p j (m i) -> p m i j", i=PACK)
+            if a < PASSES - 1:
+                grouped = held([P, PACK, P, PACK], BF16, f"w1_grouped{a}")
+                nc.scalar.copy(out=grouped[:].rearrange("p i m j -> p m i j"), in_=src)
+                nc.vector.quantize_mx(
+                    out=w1_codes[a][:].bitcast(FP8X4),
+                    scales=w1_scales[a][:],
+                    in_=grouped[:].rearrange("p i m j -> p (i m j)"),
+                )
+                for i in range(PACK):
+                    multiply_first(a, i)
+            else:
+                for u in range(2):
+                    grouped = held([P, 2, P, PACK], BF16, f"w1_grouped{a}_{u}")
+                    nc.vector.tensor_copy(
+                        out=grouped[:].rearrange("p i m j -> p m i j"), in_=src[:, :, 2 * u : 2 * u + 2, :]
+                    )
+                    for v in range(2):
+                        i = 2 * u + v
+                        cols = slice(P * i, P * (i + 1))
+                        nc.vector.quantize_mx(
+                            out=w1_codes[a][:, cols].bitcast(FP8X4),
+                            scales=w1_scales[a][:, cols],
+                            in_=grouped[:, v].rearrange("p m j -> p (m j)"),
+                        )
+                        multiply_first(a, i)
+            if a == 0:
+                nc.vector.tensor_tensor(bg[:], gain_sb[:], back_sb[:], ALU.mult)
+                nc.vector.tensor_scalar(bg_neg[:], bg[:], -1.0, None, ALU.mult)
+                nc.vector.tensor_tensor(bg_abs[:], bg[:], bg_neg[:], ALU.max)
+                nc.vector.tensor_copy(
+                    out=w4_w[:].rearrange("p (i m b) -> p m i b", i=PACK, b=2),
+                    in_=w4_w_raw[:].rearrange("p (m i b) -> p m i b", i=PACK, b=2),
+                )
+                nc.vector.tensor_copy(
+                    out=w4_s[:].rearrange("p (i m) -> p m i", i=PACK),
+                    in_=w4_s_raw[:].rearrange("p (m i) -> p m i", i=PACK),
+                )
+
+        g = [held([P, S], F32, f"g{i}") for i in range(PACK)]
+        for i in range(PACK):
+            for c in range(2):
+                nc.scalar.activation(
+                    out=g[i][:, BANK * c : BANK * (c + 1)], in_=banks[i][c][:], func=ACT.Gelu_apprx_tanh
+                )
+
+        cos_all = keep.tile([P, PACK, S], F32, name="cos_all", tag="tab_w0", align_bytes=64)
+        cos_hs = [cos_all[:, i, :] for i in range(PACK)]
+        folded = {}
+
+        def cos_fold(i):
+            folded[i] = work.tile([P, S], F32, name="fold_c")
+            nc.scalar.activation(
+                out=folded[i][:], in_=g[i][:], func=ACT.Abs, scale=bg_abs[:, i : i + 1], bias=minus_pi[:]
+            )
+
+        def cos_sin(i):
+            nc.scalar.activation(out=cos_hs[i], in_=folded[i][:], func=ACT.Sin, bias=minus_half_pi[:])
+
+        HALF = PAIRS // 2
+        x_planes = held([P, PACK, PAIRS], BF16, "x_planes")
+
+        def pair_up(i, lo, hi):
+            first = work.tile([P, hi - lo], F32, name="first")
+            pair = work.tile([P, hi - lo], F32, name="pair")
+            nc.vector.tensor_copy(first[:], g[i][:].indirect(p1[:, lo // 16 : hi // 16]))
+            nc.vector.tensor_tensor(pair[:], g[i][:].indirect(p2[:, lo // 16 : hi // 16]), first[:], ALU.add)
+            nc.scalar.activation(out=x_planes[:, i, lo:hi], in_=pair[:], func=ACT.Copy, scale=gain_sb[:, i : i + 1])
+
+        pair_up(0, 0, PAIRS)
+        cos_fold(0)
+        cos_sin(0)
+        pair_up(1, 0, PAIRS)
+        pair_up(2, 0, PAIRS)
+        cos_fold(1)
+        pair_up(3, 0, HALF)
+        pair_up(3, HALF, PAIRS)
+
+        x_grouped = [held([P, HALF, PACK], BF16, f"x_grouped{c}") for c in range(2)]
+        x_codes = [held([P, HALF], U32, f"x_codes{c}") for c in range(2)]
+        x_scales = [held([P, HALF], U8, f"x_scales{c}") for c in range(2)]
+        for c in range(2):
+            nc.vector.tensor_copy(
+                out=x_grouped[c][:].rearrange("p (m n) i -> p m i n", n=4),
+                in_=x_planes[:, :, HALF * c : HALF * (c + 1)].rearrange("p i (m n) -> p m i n", n=4),
+            )
+            nc.vector.quantize_mx(
+                out=x_codes[c][:].bitcast(FP8X4),
+                scales=x_scales[c][:],
+                in_=x_grouped[c][:].rearrange("p m i -> p (m i)"),
+            )
+        cos_sin(1)
+
+        y = [held([P, PAIRS], F32, f"y{i}") for i in range(PACK)]
+        for i in range(PACK):
+            for c in range(2):
+                acc = psum.tile([P, HALF], F32, name=f"y_acc{i}_{c}", tag=f"bank{i}_{c}")
+                nc.tensor.matmul_mx(
+                    out=acc[:],
+                    lhsT=w4_w[:, 2 * P * i : 2 * P * (i + 1)].bitcast(FP4X4),
+                    lhsT_scale=w4_s[:, P * i : P * (i + 1)],
+                    rhs=x_codes[c][:].bitcast(FP8X4),
+                    rhs_scale=x_scales[c][:],
+                    start=True,
+                    stop=True,
+                )
+                nc.scalar.copy(out=y[i][:, HALF * c : HALF * (c + 1)], in_=acc[:])
+
+        out_planes = out.rearrange("(p i) j -> p i j", i=PACK)
+        yu_all = keep.tile([P, PACK, S], F32, name="yu_all", tag="tab_w1", align_bytes=64)
+        yu = [yu_all[:, i, :] for i in range(PACK)]
+        sin_all = keep.tile([P, PACK, S], F32, name="sin_all", tag="tab_w2", align_bytes=64)
+        sin_yu = [sin_all[:, i, :] for i in range(PACK)]
+
+        def fetch(i):
+            for lo, hi in ((0, 22), (22, 44), (44, 64)):
+                nc.vector.tensor_copy(yu[i][:, 16 * lo : 16 * hi], y[i][:].indirect(p3[:, lo:hi]))
+
+        def sine(i):
+            f1 = work.tile([P, S], F32, name="fold_b")
+            f2 = work.tile([P, S], F32, name="fold_a")
+            nc.scalar.activation(out=f1[:], in_=yu[i], func=ACT.Abs, bias=minus_half_pi[:])
+            nc.scalar.activation(out=f2[:], in_=f1[:], func=ACT.Abs, bias=minus_pi[:])
+            nc.scalar.activation(out=sin_yu[i], in_=f2[:], func=ACT.Sin, bias=minus_half_pi[:])
+
+        def finish(i, edges):
+            for lo, hi in zip(edges, edges[1:]):
+                width = hi - lo
+                cols = slice(lo, hi)
+                t_cos = work.tile([P, width], F32, name="t_cos")
+                t_sin = work.tile([P, width], F32, name="t_sin")
+                result = work.tile([P, width], F32, name="result", bufs=3)
+                nc.vector.tensor_tensor(t_cos[:], yu[i][:, cols], cos_hs[i][:, cols], ALU.mult)
+                nc.vector.scalar_tensor_tensor(
+                    t_sin[:], g[i][:, cols], bg[:, i : i + 1], sin_yu[i][:, cols], ALU.mult, ALU.mult
+                )
+                nc.vector.tensor_tensor(result[:], t_cos[:], t_sin[:], ALU.add)
+                nc.sync.dma_start(out=out_planes[:, i, cols], in_=result[:])
+
+        for i in range(PACK):
+            fetch(i)
+            sine(i)
+            if i + 2 < PACK:
+                cos_fold(i + 2)
+                cos_sin(i + 2)
+        for i in range(PACK):
+            finish(i, (0, 512, 768, S) if i == PACK - 1 else (0, S))

@@ -60,16 +60,18 @@ def tile_list_slewing_play_features_kernel(
             nc.sync.dma_start(out=w1_raw[a][:], in_=rows.rearrange("(p i) r -> p i r", i=PACK))
 
         nc.sync.dma_start(idx[:], offs)
+        load_table(0)
         for q in range(4):
-            nc.scalar.dma_start(
+            nc.gpsimd.dma_start(
                 out=tab_s[32 * q : 32 * q + 4 * PASSES, :].bitcast(I32),
                 in_=tab_scales[:, 4 * q : 4 * q + 4, :].bitcast(I32),
             )
-        load_table(0)
         load_w1(0)
+        for a in range(1, PASSES):
+            load_table(a)
+            load_w1(a)
         nc.sync.dma_start(p1[:], pos1)
         nc.sync.dma_start(p2[:], pos2)
-        nc.sync.dma_start(p3[:], pos3)
         nc.sync.dma_start(out=gain_sb[:], in_=gain.rearrange("(p i) -> p i", i=PACK))
         nc.sync.dma_start(out=back_sb[:], in_=back.rearrange("(p i) -> p i", i=PACK))
         nc.sync.dma_start(out=w4_w_raw[:].bitcast(I32), in_=w4_words[0].bitcast(I32))
@@ -78,9 +80,7 @@ def tile_list_slewing_play_features_kernel(
                 out=w4_s_raw[32 * q : 32 * q + 4, :].bitcast(I32),
                 in_=w4_scales[0, 4 * q : 4 * q + 4, :].bitcast(I32),
             )
-        for a in range(1, PASSES):
-            load_table(a)
-            load_w1(a)
+        nc.sync.dma_start(p3[:], pos3)
 
         minus_half_pi = held([P, 1], F32, "minus_half_pi")
         minus_pi = held([P, 1], F32, "minus_pi")
@@ -111,7 +111,6 @@ def tile_list_slewing_play_features_kernel(
                 )
 
         bg = held([P, PACK], F32, "bg")
-        bg_neg = held([P, PACK], F32, "bg_neg")
         bg_abs = held([P, PACK], F32, "bg_abs")
         w4_w = held([P, 2 * H], U8, "w4_w")
         w4_s = held([P, H], U8, "w4_s")
@@ -144,18 +143,16 @@ def tile_list_slewing_play_features_kernel(
                             in_=grouped[:, v].rearrange("p m j -> p (m j)"),
                         )
                         multiply_first(a, i)
-            if a == 0:
-                nc.vector.tensor_tensor(bg[:], gain_sb[:], back_sb[:], ALU.mult)
-                nc.vector.tensor_scalar(bg_neg[:], bg[:], -1.0, None, ALU.mult)
-                nc.vector.tensor_tensor(bg_abs[:], bg[:], bg_neg[:], ALU.max)
-                nc.vector.tensor_copy(
-                    out=w4_w[:].rearrange("p (i m b) -> p m i b", i=PACK, b=2),
-                    in_=w4_w_raw[:].rearrange("p (m i b) -> p m i b", i=PACK, b=2),
-                )
-                nc.vector.tensor_copy(
-                    out=w4_s[:].rearrange("p (i m) -> p m i", i=PACK),
-                    in_=w4_s_raw[:].rearrange("p (m i) -> p m i", i=PACK),
-                )
+
+        nc.gpsimd.tensor_tensor(bg[:], gain_sb[:], back_sb[:], ALU.mult)
+        nc.vector.tensor_copy(
+            out=w4_w[:].bitcast(U16).rearrange("p (i m) -> p m i", i=PACK),
+            in_=w4_w_raw[:].bitcast(U16).rearrange("p (m i) -> p m i", i=PACK),
+        )
+        nc.vector.tensor_copy(
+            out=w4_s[:].rearrange("p (i m) -> p m i", i=PACK),
+            in_=w4_s_raw[:].rearrange("p (m i) -> p m i", i=PACK),
+        )
 
         g = [held([P, S], F32, f"g{i}") for i in range(PACK)]
         for i in range(PACK):
@@ -164,6 +161,7 @@ def tile_list_slewing_play_features_kernel(
                     out=g[i][:, BANK * c : BANK * (c + 1)], in_=banks[i][c][:], func=ACT.Gelu_apprx_tanh
                 )
 
+        nc.scalar.activation(out=bg_abs[:], in_=bg[:], func=ACT.Abs)
         cos_all = keep.tile([P, PACK, S], F32, name="cos_all", tag="tab_w0", align_bytes=64)
         cos_hs = [cos_all[:, i, :] for i in range(PACK)]
         folded = {}
@@ -180,36 +178,54 @@ def tile_list_slewing_play_features_kernel(
         HALF = PAIRS // 2
         x_planes = held([P, PACK, PAIRS], BF16, "x_planes")
 
-        def pair_up(i, lo, hi):
-            first = work.tile([P, hi - lo], F32, name="first")
-            pair = work.tile([P, hi - lo], F32, name="pair")
-            nc.vector.tensor_copy(first[:], g[i][:].indirect(p1[:, lo // 16 : hi // 16]))
-            nc.vector.tensor_tensor(pair[:], g[i][:].indirect(p2[:, lo // 16 : hi // 16]), first[:], ALU.add)
-            nc.scalar.activation(out=x_planes[:, i, lo:hi], in_=pair[:], func=ACT.Copy, scale=gain_sb[:, i : i + 1])
+        last = PACK - 1
 
-        pair_up(0, 0, PAIRS)
-        cos_fold(0)
-        cos_sin(0)
-        pair_up(1, 0, PAIRS)
-        pair_up(2, 0, PAIRS)
-        cos_fold(1)
-        pair_up(3, 0, HALF)
-        pair_up(3, HALF, PAIRS)
+        def pair_up(i):
+            first = work.tile([P, PAIRS], F32, name="first")
+            pair = work.tile([P, PAIRS], F32, name="pair")
+            for c in range(2):
+                nc.vector.tensor_copy(
+                    first[:, HALF * c : HALF * (c + 1)], g[i][:].indirect(p1[:, 16 * c : 16 * (c + 1)])
+                )
+            for c in range(2):
+                cols = slice(HALF * c, HALF * (c + 1))
+                nc.vector.tensor_tensor(
+                    pair[:, cols], g[i][:].indirect(p2[:, 16 * c : 16 * (c + 1)]), first[:, cols], ALU.add
+                )
+            return pair
+
+        def scale_round(engine, i, pair, lo, hi):
+            engine.tensor_scalar(x_planes[:, i, lo:hi], pair[:, lo:hi], gain_sb[:, i : i + 1], 0.0, ALU.mult, ALU.add)
 
         x_grouped = [held([P, HALF, PACK], BF16, f"x_grouped{c}") for c in range(2)]
         x_codes = [held([P, HALF], U32, f"x_codes{c}") for c in range(2)]
         x_scales = [held([P, HALF], U8, f"x_scales{c}") for c in range(2)]
-        for c in range(2):
+
+        def interleave(c):
             nc.vector.tensor_copy(
                 out=x_grouped[c][:].rearrange("p (m n) i -> p m i n", n=4),
                 in_=x_planes[:, :, HALF * c : HALF * (c + 1)].rearrange("p i (m n) -> p m i n", n=4),
             )
+
+        def quantize_x(c):
             nc.vector.quantize_mx(
                 out=x_codes[c][:].bitcast(FP8X4),
                 scales=x_scales[c][:],
                 in_=x_grouped[c][:].rearrange("p m i -> p (m i)"),
             )
-        cos_sin(1)
+
+        for i in range(PACK):
+            cos_fold(i)
+            cos_sin(i)
+        for i in range(last):
+            scale_round(nc.gpsimd, i, pair_up(i), 0, PAIRS)
+        pair = pair_up(last)
+        for c in range(2):
+            scale_round(nc.vector, last, pair, HALF * c, HALF * (c + 1))
+        for c in range(2):
+            interleave(c)
+        for c in range(2):
+            quantize_x(c)
 
         y = [held([P, PAIRS], F32, f"y{i}") for i in range(PACK)]
         for i in range(PACK):
@@ -224,7 +240,10 @@ def tile_list_slewing_play_features_kernel(
                     start=True,
                     stop=True,
                 )
-                nc.scalar.copy(out=y[i][:, HALF * c : HALF * (c + 1)], in_=acc[:])
+                if i == 0:
+                    nc.vector.tensor_copy(out=y[i][:, HALF * c : HALF * (c + 1)], in_=acc[:])
+                else:
+                    nc.scalar.copy(out=y[i][:, HALF * c : HALF * (c + 1)], in_=acc[:])
 
         out_planes = out.rearrange("(p i) j -> p i j", i=PACK)
         yu_all = keep.tile([P, PACK, S], F32, name="yu_all", tag="tab_w1", align_bytes=64)
@@ -232,9 +251,9 @@ def tile_list_slewing_play_features_kernel(
         sin_all = keep.tile([P, PACK, S], F32, name="sin_all", tag="tab_w2", align_bytes=64)
         sin_yu = [sin_all[:, i, :] for i in range(PACK)]
 
-        def fetch(i):
-            for lo, hi in ((0, 22), (22, 44), (44, 64)):
-                nc.vector.tensor_copy(yu[i][:, 16 * lo : 16 * hi], y[i][:].indirect(p3[:, lo:hi]))
+        def fetch(i, c):
+            for lo in (32 * c, 32 * c + 16):
+                nc.vector.tensor_copy(yu[i][:, 16 * lo : 16 * (lo + 16)], y[i][:].indirect(p3[:, lo : lo + 16]))
 
         def sine(i):
             f1 = work.tile([P, S], F32, name="fold_b")
@@ -243,25 +262,26 @@ def tile_list_slewing_play_features_kernel(
             nc.scalar.activation(out=f2[:], in_=f1[:], func=ACT.Abs, bias=minus_pi[:])
             nc.scalar.activation(out=sin_yu[i], in_=f2[:], func=ACT.Sin, bias=minus_half_pi[:])
 
+        t_cos = [work.tile([P, S], F32, name=f"t_cos{i}", bufs=1) for i in range(PACK)]
+
         def finish(i, edges):
-            for lo, hi in zip(edges, edges[1:]):
-                width = hi - lo
-                cols = slice(lo, hi)
-                t_cos = work.tile([P, width], F32, name="t_cos")
-                t_sin = work.tile([P, width], F32, name="t_sin")
-                result = work.tile([P, width], F32, name="result", bufs=3)
-                nc.vector.tensor_tensor(t_cos[:], yu[i][:, cols], cos_hs[i][:, cols], ALU.mult)
+            pieces = [slice(lo, hi) for lo, hi in zip(edges, edges[1:])]
+            t_sin = work.tile([P, S], F32, name="t_sin")
+            result = work.tile([P, S], F32, name="result", bufs=3)
+            for cols in pieces:
                 nc.vector.scalar_tensor_tensor(
-                    t_sin[:], g[i][:, cols], bg[:, i : i + 1], sin_yu[i][:, cols], ALU.mult, ALU.mult
+                    t_sin[:, cols], g[i][:, cols], bg[:, i : i + 1], sin_yu[i][:, cols], ALU.mult, ALU.mult
                 )
-                nc.vector.tensor_tensor(result[:], t_cos[:], t_sin[:], ALU.add)
-                nc.sync.dma_start(out=out_planes[:, i, cols], in_=result[:])
+            for cols in pieces:
+                nc.vector.tensor_tensor(result[:, cols], t_cos[i][:, cols], t_sin[:, cols], ALU.add)
+                nc.sync.dma_start(out=out_planes[:, i, cols], in_=result[:, cols])
 
         for i in range(PACK):
-            fetch(i)
+            for c in range(2):
+                fetch(i, c)
+                cols = slice(BANK * c, BANK * (c + 1))
+                engine = nc.vector if (i, c) == (last, 1) else nc.gpsimd
+                engine.tensor_tensor(t_cos[i][:, cols], yu[i][:, cols], cos_hs[i][:, cols], ALU.mult)
             sine(i)
-            if i + 2 < PACK:
-                cos_fold(i + 2)
-                cos_sin(i + 2)
         for i in range(PACK):
-            finish(i, (0, 512, 768, S) if i == PACK - 1 else (0, S))
+            finish(i, (0, 512, 768, S) if i == last else (0, 512, S))

import math
from contextlib import ExitStack

import concourse.mybir as mybir

K, T, S, H, PAIRS = 1536, 4096, 1024, 512, 512
FLOPS = 2 * K * H * S + 2 * H * H * PAIRS

F32 = mybir.dt.float32
BF16 = mybir.dt.bfloat16
I32 = mybir.dt.int32
U32 = mybir.dt.uint32
U16 = mybir.dt.uint16
U8 = mybir.dt.uint8
FP8X4 = mybir.dt.float8_e4m3fn_x4
FP4X4 = mybir.dt.float4_e2m1fn_x4
ACT = mybir.ActivationFunctionType
ALU = mybir.AluOpType

P = 128
PACK = 4
PASSES = K // (P * PACK)
BANK = 512


def tile_list_slewing_play_features_kernel(
    tc, tab_words, tab_scales, offs, w1, gain, pos1, pos2, w4_words, w4_scales, pos3, back, out
):
    nc = tc.nc
    with ExitStack() as ctx:
        keep = ctx.enter_context(tc.tile_pool(name="keep", bufs=1))
        psum = ctx.enter_context(tc.psum_pool(name="psum", bufs=1))
        work = ctx.enter_context(tc.tile_pool(name="work", bufs=2))

        def held(shape, dtype, name):
            return keep.tile(shape, dtype, name=name, align_bytes=64)

        idx = held([P, S // 16], U16, "idx")
        p1 = held([P, PAIRS // 16], U16, "p1")
        p2 = held([P, PAIRS // 16], U16, "p2")
        p3 = held([P, S // 16], U16, "p3")
        tab_w = [keep.tile([P, T], U32, name=f"tab_w{a}", tag=f"tab_w{a}", align_bytes=64) for a in range(PASSES)]
        tab_s = held([P, T], U8, "tab_s")
        w1_raw = [held([P, PACK, H], F32, f"w1_raw{a}") for a in range(PASSES)]
        gain_sb = held([P, PACK], F32, "gain_sb")
        back_sb = held([P, PACK], F32, "back_sb")
        w4_w_raw = held([P, 2 * H], U8, "w4_w_raw")
        w4_s_raw = held([P, H], U8, "w4_s_raw")

        nc.vector.memset(tab_s[:].bitcast(I32), 0)
        nc.vector.memset(w4_s_raw[:].bitcast(I32), 0)

        def load_table(a):
            nc.sync.dma_start(
                out=tab_w[a][:].bitcast(I32), in_=tab_words[a].rearrange("p n i -> p (n i)").bitcast(I32)
            )

        def load_w1(a):
            rows = w1[a * P * PACK : (a + 1) * P * PACK, :]
            nc.sync.dma_start(out=w1_raw[a][:], in_=rows.rearrange("(p i) r -> p i r", i=PACK))

        nc.sync.dma_start(idx[:], offs)
        load_table(0)
        for q in range(4):
            nc.gpsimd.dma_start(
                out=tab_s[32 * q : 32 * q + 4 * PASSES, :].bitcast(I32),
                in_=tab_scales[:, 4 * q : 4 * q + 4, :].bitcast(I32),
            )
        load_w1(0)
        for a in range(1, PASSES):
            load_table(a)
            load_w1(a)
        nc.sync.dma_start(p1[:], pos1)
        nc.sync.dma_start(p2[:], pos2)
        nc.sync.dma_start(out=gain_sb[:], in_=gain.rearrange("(p i) -> p i", i=PACK))
        nc.sync.dma_start(out=back_sb[:], in_=back.rearrange("(p i) -> p i", i=PACK))
        nc.sync.dma_start(out=w4_w_raw[:].bitcast(I32), in_=w4_words[0].bitcast(I32))
        for q in range(4):
            nc.sync.dma_start(
                out=w4_s_raw[32 * q : 32 * q + 4, :].bitcast(I32),
                in_=w4_scales[0, 4 * q : 4 * q + 4, :].bitcast(I32),
            )
        nc.sync.dma_start(p3[:], pos3)

        minus_half_pi = held([P, 1], F32, "minus_half_pi")
        minus_pi = held([P, 1], F32, "minus_pi")
        one = held([P, 1], F32, "one")
        nc.vector.memset(one[:], 1.0)
        nc.vector.tensor_scalar(minus_half_pi[:], one[:], -math.pi / 2, None, ALU.mult)
        nc.vector.tensor_scalar(minus_pi[:], one[:], -math.pi, None, ALU.mult)

        got_s = held([P, S], U8, "got_s")
        nc.vector.tensor_copy(got_s[:], tab_s[:].indirect(idx[:]))
        got_w = [held([P, S], U32, f"got_w{a}") for a in range(PASSES)]
        w1_codes = [held([P, H], U32, f"w1_codes{a}") for a in range(PASSES)]
        w1_scales = [held([P, H], U8, f"w1_scales{a}") for a in range(PASSES)]
        banks = [[psum.tile([P, BANK], F32, name=f"e{i}_{c}", tag=f"bank{i}_{c}") for c in range(2)] for i in range(PACK)]

        def multiply_first(a, i):
            cols = slice(P * i, P * (i + 1))
            for c in range(2):
                ent = slice(BANK * c, BANK * (c + 1))
                nc.tensor.matmul_mx(
                    out=banks[i][c][:],
                    lhsT=w1_codes[a][:, cols].bitcast(FP8X4),
                    lhsT_scale=w1_scales[a][:, cols],
                    rhs=got_w[a][:, ent].bitcast(FP8X4),
                    rhs_scale=got_s[4 * a : P, ent],
                    start=(a == 0),
                    stop=(a == PASSES - 1),
                )

        bg = held([P, PACK], F32, "bg")
        bg_abs = held([P, PACK], F32, "bg_abs")
        w4_w = held([P, 2 * H], U8, "w4_w")
        w4_s = held([P, H], U8, "w4_s")

        for a in range(PASSES):
            nc.vector.tensor_copy(got_w[a][:], tab_w[a][:].indirect(idx[:]))
            src = w1_raw[a][:].rearrange("p j (m i) -> p m i j", i=PACK)
            if a < PASSES - 1:
                grouped = held([P, PACK, P, PACK], BF16, f"w1_grouped{a}")
                nc.scalar.copy(out=grouped[:].rearrange("p i m j -> p m i j"), in_=src)
                nc.vector.quantize_mx(
                    out=w1_codes[a][:].bitcast(FP8X4),
                    scales=w1_scales[a][:],
                    in_=grouped[:].rearrange("p i m j -> p (i m j)"),
                )
                for i in range(PACK):
                    multiply_first(a, i)
            else:
                for u in range(2):
                    grouped = held([P, 2, P, PACK], BF16, f"w1_grouped{a}_{u}")
                    nc.vector.tensor_copy(
                        out=grouped[:].rearrange("p i m j -> p m i j"), in_=src[:, :, 2 * u : 2 * u + 2, :]
                    )
                    for v in range(2):
                        i = 2 * u + v
                        cols = slice(P * i, P * (i + 1))
                        nc.vector.quantize_mx(
                            out=w1_codes[a][:, cols].bitcast(FP8X4),
                            scales=w1_scales[a][:, cols],
                            in_=grouped[:, v].rearrange("p m j -> p (m j)"),
                        )
                        multiply_first(a, i)

        nc.gpsimd.tensor_tensor(bg[:], gain_sb[:], back_sb[:], ALU.mult)
        nc.vector.tensor_copy(
            out=w4_w[:].bitcast(U16).rearrange("p (i m) -> p m i", i=PACK),
            in_=w4_w_raw[:].bitcast(U16).rearrange("p (m i) -> p m i", i=PACK),
        )
        nc.vector.tensor_copy(
            out=w4_s[:].rearrange("p (i m) -> p m i", i=PACK),
            in_=w4_s_raw[:].rearrange("p (m i) -> p m i", i=PACK),
        )

        g = [held([P, S], F32, f"g{i}") for i in range(PACK)]
        for i in range(PACK):
            for c in range(2):
                nc.scalar.activation(
                    out=g[i][:, BANK * c : BANK * (c + 1)], in_=banks[i][c][:], func=ACT.Gelu_apprx_tanh
                )

        nc.scalar.activation(out=bg_abs[:], in_=bg[:], func=ACT.Abs)
        cos_all = keep.tile([P, PACK, S], F32, name="cos_all", tag="tab_w0", align_bytes=64)
        cos_hs = [cos_all[:, i, :] for i in range(PACK)]
        folded = {}

        def cos_fold(i):
            folded[i] = work.tile([P, S], F32, name="fold_c")
            nc.scalar.activation(
                out=folded[i][:], in_=g[i][:], func=ACT.Abs, scale=bg_abs[:, i : i + 1], bias=minus_pi[:]
            )

        def cos_sin(i):
            nc.scalar.activation(out=cos_hs[i], in_=folded[i][:], func=ACT.Sin, bias=minus_half_pi[:])

        HALF = PAIRS // 2
        x_planes = held([P, PACK, PAIRS], BF16, "x_planes")

        last = PACK - 1

        def pair_up(i):
            first = work.tile([P, PAIRS], F32, name="first")
            pair = work.tile([P, PAIRS], F32, name="pair")
            for c in range(2):
                nc.vector.tensor_copy(
                    first[:, HALF * c : HALF * (c + 1)], g[i][:].indirect(p1[:, 16 * c : 16 * (c + 1)])
                )
            for c in range(2):
                cols = slice(HALF * c, HALF * (c + 1))
                nc.vector.tensor_tensor(
                    pair[:, cols], g[i][:].indirect(p2[:, 16 * c : 16 * (c + 1)]), first[:, cols], ALU.add
                )
            return pair

        def scale_round(engine, i, pair, lo, hi):
            engine.tensor_scalar(x_planes[:, i, lo:hi], pair[:, lo:hi], gain_sb[:, i : i + 1], 0.0, ALU.mult, ALU.add)

        x_grouped = [held([P, HALF, PACK], BF16, f"x_grouped{c}") for c in range(2)]
        x_codes = [held([P, HALF], U32, f"x_codes{c}") for c in range(2)]
        x_scales = [held([P, HALF], U8, f"x_scales{c}") for c in range(2)]

        def interleave(c):
            nc.vector.tensor_copy(
                out=x_grouped[c][:].rearrange("p (m n) i -> p m i n", n=4),
                in_=x_planes[:, :, HALF * c : HALF * (c + 1)].rearrange("p i (m n) -> p m i n", n=4),
            )

        def quantize_x(c):
            nc.vector.quantize_mx(
                out=x_codes[c][:].bitcast(FP8X4),
                scales=x_scales[c][:],
                in_=x_grouped[c][:].rearrange("p m i -> p (m i)"),
            )

        for i in range(PACK):
            cos_fold(i)
            cos_sin(i)
        for i in range(last):
            scale_round(nc.gpsimd, i, pair_up(i), 0, PAIRS)
        pair = pair_up(last)
        for c in range(2):
            scale_round(nc.vector, last, pair, HALF * c, HALF * (c + 1))
        for c in range(2):
            interleave(c)
        for c in range(2):
            quantize_x(c)

        y = [held([P, PAIRS], F32, f"y{i}") for i in range(PACK)]
        for i in range(PACK):
            for c in range(2):
                acc = psum.tile([P, HALF], F32, name=f"y_acc{i}_{c}", tag=f"bank{i}_{c}")
                nc.tensor.matmul_mx(
                    out=acc[:],
                    lhsT=w4_w[:, 2 * P * i : 2 * P * (i + 1)].bitcast(FP4X4),
                    lhsT_scale=w4_s[:, P * i : P * (i + 1)],
                    rhs=x_codes[c][:].bitcast(FP8X4),
                    rhs_scale=x_scales[c][:],
                    start=True,
                    stop=True,
                )
                if i == 0:
                    nc.vector.tensor_copy(out=y[i][:, HALF * c : HALF * (c + 1)], in_=acc[:])
                else:
                    nc.scalar.copy(out=y[i][:, HALF * c : HALF * (c + 1)], in_=acc[:])

        out_planes = out.rearrange("(p i) j -> p i j", i=PACK)
        yu_all = keep.tile([P, PACK, S], F32, name="yu_all", tag="tab_w1", align_bytes=64)
        yu = [yu_all[:, i, :] for i in range(PACK)]
        sin_all = keep.tile([P, PACK, S], F32, name="sin_all", tag="tab_w2", align_bytes=64)
        sin_yu = [sin_all[:, i, :] for i in range(PACK)]

        def fetch(i, c):
            for lo in (32 * c, 32 * c + 16):
                nc.vector.tensor_copy(yu[i][:, 16 * lo : 16 * (lo + 16)], y[i][:].indirect(p3[:, lo : lo + 16]))

        def sine(i):
            f1 = work.tile([P, S], F32, name="fold_b")
            f2 = work.tile([P, S], F32, name="fold_a")
            nc.scalar.activation(out=f1[:], in_=yu[i], func=ACT.Abs, bias=minus_half_pi[:])
            nc.scalar.activation(out=f2[:], in_=f1[:], func=ACT.Abs, bias=minus_pi[:])
            nc.scalar.activation(out=sin_yu[i], in_=f2[:], func=ACT.Sin, bias=minus_half_pi[:])

        t_cos = [work.tile([P, S], F32, name=f"t_cos{i}", bufs=1) for i in range(PACK)]

        def finish(i, edges):
            pieces = [slice(lo, hi) for lo, hi in zip(edges, edges[1:])]
            t_sin = work.tile([P, S], F32, name="t_sin")
            result = work.tile([P, S], F32, name="result", bufs=3)
            for cols in pieces:
                nc.vector.scalar_tensor_tensor(
                    t_sin[:, cols], g[i][:, cols], bg[:, i : i + 1], sin_yu[i][:, cols], ALU.mult, ALU.mult
                )
            for cols in pieces:
                nc.vector.tensor_tensor(result[:, cols], t_cos[i][:, cols], t_sin[:, cols], ALU.add)
                nc.sync.dma_start(out=out_planes[:, i, cols], in_=result[:, cols])

        for i in range(PACK):
            for c in range(2):
                fetch(i, c)
                cols = slice(BANK * c, BANK * (c + 1))
                engine = nc.vector if (i, c) == (last, 1) else nc.gpsimd
                engine.tensor_tensor(t_cos[i][:, cols], yu[i][:, cols], cos_hs[i][:, cols], ALU.mult)
            sine(i)
        for i in range(PACK):
            finish(i, (0, 512, 768, S) if i == last else (0, 512, S))
